import numpy as np, ml_dtypes
CORES = [2,10,18,26,34,42,50,58]
N = 8
def setup_inputs(rng):
    return {"x": rng.standard_normal((N, 128, 2048), dtype=np.float32).astype(ml_dtypes.bfloat16)}
def reference(x):
    s = np.cumsum(x.astype(np.float64), axis=0)
    return {"y": s.astype(x.dtype)}

@@ -1,0 +1,28 @@
+from concourse.mybir import AluOpType
+
+SCRATCH = {
+    "xs": ("sbuf", [128, 2048], "bfloat16"),
+    "land": ("sbuf", [128, 2048], "bfloat16"),
+}
+SEMAPHORES = ["loaded", "added", "stored", "arrived", "sent"]
+
+
+def rank_program(g, core, T, topo):
+    rank = T.rank_of(core)
+    if rank is None:
+        return
+    n = len(T.cores)
+    g.dma_start(T.xs[:], T.x[:]).then_inc(T.sem.loaded, 16)
+    g.wait_ge(T.sem.loaded, 16)
+    if rank > 0:
+        g.wait_ge(T.sem.arrived, 8)
+        g.dma_start(T.xs[:], T.land[:], accum_op=AluOpType.add, max_dma_last_dim=4096).then_inc(T.sem.added, 16)
+        g.wait_ge(T.sem.added, 16)
+    if rank < n - 1:
+        dst = T.cores[rank + 1]
+        rid, pid, se = topo.addr(dst)
+        g.remote_dma(T.land[:], T.xs[:], T.sem.arrived, T.sem.sent, pid, rid, topo.mask(core, dst))
+    g.dma_start(T.y[:], T.xs[:]).then_inc(T.sem.stored, 16)
+    g.wait_ge(T.sem.stored, 16)
+    if rank < n - 1:
+        g.wait_ge(T.sem.sent, 8)

@@ -1,28 +1,77 @@
+from concourse.bass import DstId, RemoteDMATransfer
 from concourse.mybir import AluOpType
 
+NP = 8
+W = 256
 SCRATCH = {
-    "xs": ("sbuf", [128, 2048], "bfloat16"),
-    "land": ("sbuf", [128, 2048], "bfloat16"),
+    "xd": ("dram", [NP, 128, W], "bfloat16"),
+    "gath": ("dram", [7, 128, W], "bfloat16"),
+    "land": ("dram", [NP, 128, W], "bfloat16"),
 }
-SEMAPHORES = ["loaded", "added", "stored", "arrived", "sent"]
+SEMAPHORES = ["loaded", "copied", "added", "got", "arrived", "sent"]
+ONCHIP = 0xFF00
+
+
+def owner_core(o):
+    return 8 * o + 3
 
 
 def rank_program(g, core, T, topo):
     rank = T.rank_of(core)
-    if rank is None:
-        return
     n = len(T.cores)
-    g.dma_start(T.xs[:], T.x[:]).then_inc(T.sem.loaded, 16)
-    g.wait_ge(T.sem.loaded, 16)
-    if rank > 0:
-        g.wait_ge(T.sem.arrived, 8)
-        g.dma_start(T.xs[:], T.land[:], accum_op=AluOpType.add, max_dma_last_dim=4096).then_inc(T.sem.added, 16)
-        g.wait_ge(T.sem.added, 16)
-    if rank < n - 1:
-        dst = T.cores[rank + 1]
+    if rank is not None:
+        if rank < n - 1:
+            g.dma_start(T.xd[:], T.x[:]).then_inc(T.sem.loaded, 16)
+        g.dma_start(T.y[:], T.x[:]).then_inc(T.sem.copied, 16)
+        sent = 0
+        if rank < n - 1:
+            g.wait_ge(T.sem.loaded, 16)
+            trs = []
+            e = 0
+            for o in range(NP):
+                dst = owner_core(o)
+                rid, pid, se = topo.addr(dst)
+                if topo.chip(dst) == topo.chip(core):
+                    m = ONCHIP
+                    sent += 8
+                else:
+                    m = 1 << e
+                    e += 1
+                    sent += 1
+                trs.append(RemoteDMATransfer(dst_ids=[DstId(rid=rid, pnc=pid)], dma_engine_mask=m,
+                                             remote_sem=T.sem.got, src=T.xd[o], dst=T.gath[rank]))
+            g.remote_dma_fused(trs, local_sem=T.sem.sent)
+        g.wait_ge(T.sem.copied, 16)
+        if rank > 0:
+            g.wait_ge(T.sem.arrived, 7 + 8)
+            g.dma_start(T.y[:], T.land[:], accum_op=AluOpType.add, max_dma_last_dim=4096).then_inc(T.sem.added, 16)
+            g.wait_ge(T.sem.added, 16)
+        if sent:
+            g.wait_ge(T.sem.sent, sent)
+        return
+    if core % 8 != 3:
+        return
+    o = core // 8
+    g.wait_ge(T.sem.got, sum(8 if r == o else 1 for r in range(n - 1)))
+    trs = []
+    e = 0
+    sent = 0
+    for r in range(1, n):
+        dst = T.cores[r]
         rid, pid, se = topo.addr(dst)
-        g.remote_dma(T.land[:], T.xs[:], T.sem.arrived, T.sem.sent, pid, rid, topo.mask(core, dst))
-    g.dma_start(T.y[:], T.xs[:]).then_inc(T.sem.stored, 16)
-    g.wait_ge(T.sem.stored, 16)
-    if rank < n - 1:
-        g.wait_ge(T.sem.sent, 8)
+        if topo.chip(dst) == topo.chip(core):
+            m = ONCHIP
+            sent += 8
+        else:
+            m = 1 << e
+            e += 1
+            sent += 1
+        if r == 1:
+            trs.append(RemoteDMATransfer(dst_ids=[DstId(rid=rid, pnc=pid)], dma_engine_mask=m,
+                                         remote_sem=T.sem.arrived, src=T.gath[0], dst=T.land[o]))
+        else:
+            trs.append(RemoteDMATransfer(dst_ids=[DstId(rid=rid, pnc=pid)], dma_engine_mask=m,
+                                         remote_sem=T.sem.arrived, srcs=[T.gath[j] for j in range(r)],
+                                         dsts=[T.land[o]], alu_op=1))
+    g.remote_dma_fused(trs, local_sem=T.sem.sent)
+    g.wait_ge(T.sem.sent, sent)

@@ -1,77 +1,98 @@
 from concourse.bass import DstId, RemoteDMATransfer
 from concourse.mybir import AluOpType
 
-NP = 8
-W = 256
-SCRATCH = {
-    "xd": ("dram", [NP, 128, W], "bfloat16"),
-    "gath": ("dram", [7, 128, W], "bfloat16"),
-    "land": ("dram", [NP, 128, W], "bfloat16"),
-}
-SEMAPHORES = ["loaded", "copied", "added", "got", "arrived", "sent"]
+OWN = [3, 6, 7]
+WID = [96, 80, 80]
+ROWS = [8 * w // 16 for w in WID]
+BASE = [sum(ROWS[:i]) for i in range(len(WID))]
+K = len(OWN)
+SCRATCH = {}
+for i in range(K):
+    SCRATCH["xd%d" % i] = ("dram", [8, 128, WID[i]], "bfloat16")
+    SCRATCH["gath%d" % i] = ("dram", [7, 128, WID[i]], "bfloat16")
+    SCRATCH["land%d" % i] = ("dram", [8, 128, WID[i]], "bfloat16")
+SEMAPHORES = ["copied", "added", "got", "sent"] + ["loaded%d" % i for i in range(K)] + ["arrived%d" % i for i in range(K)]
 ONCHIP = 0xFF00
 
 
-def owner_core(o):
-    return 8 * o + 3
+def bits(m):
+    return bin(m).count("1")
+
+
+def sched(o):
+    off = [r for r in range(7, 0, -1) if r != o]
+    a = [(off[0], 0x0F), (off[1], 0xF0)]
+    if o >= 1:
+        a.append((o, ONCHIP))
+    rest = off[2:]
+    cnt = [2, 2, 2, 1, 1] if len(rest) == 5 else [2, 2, 2, 2]
+    jobs = sorted(zip(rest, cnt), key=lambda t: -t[0] / t[1])
+    order = [4, 5, 6, 7, 0, 1, 2, 3]
+    b = []
+    p = 0
+    for r, c in jobs:
+        m = 0
+        for q in range(c):
+            m |= 1 << order[p]
+            p += 1
+        b.append((r, m))
+    return [a, b]
 
 
 def rank_program(g, core, T, topo):
     rank = T.rank_of(core)
     n = len(T.cores)
+    xd = [T.xd0, T.xd1, T.xd2]
+    gath = [T.gath0, T.gath1, T.gath2]
+    land = [T.land0, T.land1, T.land2]
+    loaded = [T.sem.loaded0, T.sem.loaded1, T.sem.loaded2]
+    arrived = [T.sem.arrived0, T.sem.arrived1, T.sem.arrived2]
     if rank is not None:
-        if rank < n - 1:
-            g.dma_start(T.xd[:], T.x[:]).then_inc(T.sem.loaded, 16)
-        g.dma_start(T.y[:], T.x[:]).then_inc(T.sem.copied, 16)
         sent = 0
         if rank < n - 1:
-            g.wait_ge(T.sem.loaded, 16)
-            trs = []
-            e = 0
-            for o in range(NP):
-                dst = owner_core(o)
-                rid, pid, se = topo.addr(dst)
-                if topo.chip(dst) == topo.chip(core):
-                    m = ONCHIP
-                    sent += 8
-                else:
-                    m = 1 << e
-                    e += 1
-                    sent += 1
-                trs.append(RemoteDMATransfer(dst_ids=[DstId(rid=rid, pnc=pid)], dma_engine_mask=m,
-                                             remote_sem=T.sem.got, src=T.xd[o], dst=T.gath[rank]))
-            g.remote_dma_fused(trs, local_sem=T.sem.sent)
+            for i in range(K):
+                g.dma_start(xd[i][:], T.x[BASE[i]:BASE[i] + ROWS[i], :]).then_inc(loaded[i], 16)
+            for i in range(K):
+                g.wait_ge(loaded[i], 16)
+                trs = []
+                eng = [e for e in range(8) if e != i]
+                for o in range(8):
+                    dst = 8 * o + OWN[i]
+                    rid, pid, se = topo.addr(dst)
+                    m = ONCHIP if o == topo.chip(core) else 1 << eng.pop(0)
+                    sent += bits(m)
+                    trs.append(RemoteDMATransfer(dst_ids=[DstId(rid=rid, pnc=pid)], dma_engine_mask=m,
+                                                 remote_sem=T.sem.got, src=xd[i][o], dst=gath[i][rank]))
+                g.remote_dma_fused(trs, local_sem=T.sem.sent)
+        g.dma_start(T.y[:], T.x[:]).then_inc(T.sem.copied, 16)
         g.wait_ge(T.sem.copied, 16)
         if rank > 0:
-            g.wait_ge(T.sem.arrived, 7 + 8)
-            g.dma_start(T.y[:], T.land[:], accum_op=AluOpType.add, max_dma_last_dim=4096).then_inc(T.sem.added, 16)
-            g.wait_ge(T.sem.added, 16)
+            need = sum(bits(m) for o in range(8) for call in sched(o) for r, m in call if r == rank)
+            for i in range(K):
+                g.wait_ge(arrived[i], need)
+                g.dma_start(T.y[BASE[i]:BASE[i] + ROWS[i], :], land[i][:], accum_op=AluOpType.add,
+                            max_dma_last_dim=4096).then_inc(T.sem.added, 16)
+            g.wait_ge(T.sem.added, 16 * K)
         if sent:
             g.wait_ge(T.sem.sent, sent)
         return
-    if core % 8 != 3:
+    if core % 8 not in OWN:
         return
+    i = OWN.index(core % 8)
     o = core // 8
     g.wait_ge(T.sem.got, sum(8 if r == o else 1 for r in range(n - 1)))
-    trs = []
-    e = 0
     sent = 0
-    for r in range(1, n):
-        dst = T.cores[r]
-        rid, pid, se = topo.addr(dst)
-        if topo.chip(dst) == topo.chip(core):
-            m = ONCHIP
-            sent += 8
-        else:
-            m = 1 << e
-            e += 1
-            sent += 1
-        if r == 1:
-            trs.append(RemoteDMATransfer(dst_ids=[DstId(rid=rid, pnc=pid)], dma_engine_mask=m,
-                                         remote_sem=T.sem.arrived, src=T.gath[0], dst=T.land[o]))
-        else:
-            trs.append(RemoteDMATransfer(dst_ids=[DstId(rid=rid, pnc=pid)], dma_engine_mask=m,
-                                         remote_sem=T.sem.arrived, srcs=[T.gath[j] for j in range(r)],
-                                         dsts=[T.land[o]], alu_op=1))
-    g.remote_dma_fused(trs, local_sem=T.sem.sent)
+    for call in sched(o):
+        trs = []
+        for r, m in call:
+            rid, pid, se = topo.addr(T.cores[r])
+            sent += bits(m)
+            if r == 1:
+                trs.append(RemoteDMATransfer(dst_ids=[DstId(rid=rid, pnc=pid)], dma_engine_mask=m,
+                                             remote_sem=arrived[i], src=gath[i][0], dst=land[i][o]))
+            else:
+                trs.append(RemoteDMATransfer(dst_ids=[DstId(rid=rid, pnc=pid)], dma_engine_mask=m,
+                                             remote_sem=arrived[i], srcs=[gath[i][j] for j in range(r)],
+                                             dsts=[land[i][o]], alu_op=1))
+        g.remote_dma_fused(trs, local_sem=T.sem.sent)
     g.wait_ge(T.sem.sent, sent)

@@ -2,8 +2,9 @@ from concourse.bass import DstId, RemoteDMATransfer
 from concourse.mybir import AluOpType
 
 OWN = [3, 6, 7]
-WID = [96, 80, 80]
-ROWS = [8 * w // 16 for w in WID]
+REL = [0, 4, 5]
+WID = [86, 86, 84]
+ROWS = [w // 2 for w in WID]
 BASE = [sum(ROWS[:i]) for i in range(len(WID))]
 K = len(OWN)
 SCRATCH = {}
@@ -11,32 +12,34 @@ for i in range(K):
     SCRATCH["xd%d" % i] = ("dram", [8, 128, WID[i]], "bfloat16")
     SCRATCH["gath%d" % i] = ("dram", [7, 128, WID[i]], "bfloat16")
     SCRATCH["land%d" % i] = ("dram", [8, 128, WID[i]], "bfloat16")
-SEMAPHORES = ["copied", "added", "got", "sent"] + ["loaded%d" % i for i in range(K)] + ["arrived%d" % i for i in range(K)]
-ONCHIP = 0xFF00
+    SCRATCH["rel%d" % i] = ("dram", [2, 128, WID[i]], "bfloat16")
+SEMAPHORES = (["copied", "added", "got", "sent", "relin"] + ["loaded%d" % i for i in range(K)]
+              + ["arrived%d" % i for i in range(K)])
+LO, HI = 0x0F, 0xF0
 
 
 def bits(m):
     return bin(m).count("1")
 
 
+def relayed(o):
+    same = [r for r in range(7, 0, -1) if r % 2 == o % 2 and r != o]
+    if o % 2 == 1 and same[0] == 7:
+        same = same[1:]
+    return same[:2]
+
+
 def sched(o):
-    off = [r for r in range(7, 0, -1) if r != o]
-    a = [(off[0], 0x0F), (off[1], 0xF0)]
+    rl = relayed(o)
+    d = [r for r in range(7, 0, -1) if r != o and r not in rl]
+    a = [(d[0], LO, None), (d[1], HI, None), (rl[0], 0x0F00, 0), (rl[1], 0xF000, 1)]
+    b = [(d[2], HI, None), (d[3], LO, None)]
     if o >= 1:
-        a.append((o, ONCHIP))
-    rest = off[2:]
-    cnt = [2, 2, 2, 1, 1] if len(rest) == 5 else [2, 2, 2, 2]
-    jobs = sorted(zip(rest, cnt), key=lambda t: -t[0] / t[1])
-    order = [4, 5, 6, 7, 0, 1, 2, 3]
-    b = []
-    p = 0
-    for r, c in jobs:
-        m = 0
-        for q in range(c):
-            m |= 1 << order[p]
-            p += 1
-        b.append((r, m))
-    return [a, b]
+        b.append((o, 0xFF00, None))
+    calls = [a, b]
+    if len(d) > 4:
+        calls.append([(d[4], HI, None)])
+    return calls
 
 
 def rank_program(g, core, T, topo):
@@ -45,8 +48,15 @@ def rank_program(g, core, T, topo):
     xd = [T.xd0, T.xd1, T.xd2]
     gath = [T.gath0, T.gath1, T.gath2]
     land = [T.land0, T.land1, T.land2]
+    rel = [T.rel0, T.rel1, T.rel2]
     loaded = [T.sem.loaded0, T.sem.loaded1, T.sem.loaded2]
     arrived = [T.sem.arrived0, T.sem.arrived1, T.sem.arrived2]
+    o = topo.chip(core)
+
+    def to(dst):
+        rid, pid, se = topo.addr(dst)
+        return [DstId(rid=rid, pnc=pid)]
+
     if rank is not None:
         sent = 0
         if rank < n - 1:
@@ -56,18 +66,16 @@ def rank_program(g, core, T, topo):
                 g.wait_ge(loaded[i], 16)
                 trs = []
                 eng = [e for e in range(8) if e != i]
-                for o in range(8):
-                    dst = 8 * o + OWN[i]
-                    rid, pid, se = topo.addr(dst)
-                    m = ONCHIP if o == topo.chip(core) else 1 << eng.pop(0)
+                for c in range(8):
+                    m = 0xFF00 if c == o else 1 << eng.pop(0)
                     sent += bits(m)
-                    trs.append(RemoteDMATransfer(dst_ids=[DstId(rid=rid, pnc=pid)], dma_engine_mask=m,
-                                                 remote_sem=T.sem.got, src=xd[i][o], dst=gath[i][rank]))
+                    trs.append(RemoteDMATransfer(dst_ids=to(8 * c + OWN[i]), dma_engine_mask=m,
+                                                 remote_sem=T.sem.got, src=xd[i][c], dst=gath[i][rank]))
                 g.remote_dma_fused(trs, local_sem=T.sem.sent)
         g.dma_start(T.y[:], T.x[:]).then_inc(T.sem.copied, 16)
         g.wait_ge(T.sem.copied, 16)
         if rank > 0:
-            need = sum(bits(m) for o in range(8) for call in sched(o) for r, m in call if r == rank)
+            need = sum(bits(m) for c in range(8) for call in sched(c) for r, m, s in call if r == rank)
             for i in range(K):
                 g.wait_ge(arrived[i], need)
                 g.dma_start(T.y[BASE[i]:BASE[i] + ROWS[i], :], land[i][:], accum_op=AluOpType.add,
@@ -76,23 +84,35 @@ def rank_program(g, core, T, topo):
         if sent:
             g.wait_ge(T.sem.sent, sent)
         return
-    if core % 8 not in OWN:
+
+    if core % 8 in OWN:
+        i = OWN.index(core % 8)
+        g.wait_ge(T.sem.got, sum(8 if r == o else 1 for r in range(n - 1)))
+        sent = 0
+        for call in sched(o):
+            trs = []
+            for r, m, s in call:
+                sent += bits(m)
+                if s is None:
+                    where, sem, out = to(T.cores[r]), arrived[i], land[i][o]
+                else:
+                    where, sem, out = to(8 * o + REL[i]), T.sem.relin, rel[i][s]
+                if r == 1:
+                    trs.append(RemoteDMATransfer(dst_ids=where, dma_engine_mask=m, remote_sem=sem,
+                                                 src=gath[i][0], dst=out))
+                else:
+                    trs.append(RemoteDMATransfer(dst_ids=where, dma_engine_mask=m, remote_sem=sem,
+                                                 srcs=[gath[i][j] for j in range(r)], dsts=[out], alu_op=1))
+            g.remote_dma_fused(trs, local_sem=T.sem.sent)
+        g.wait_ge(T.sem.sent, sent)
         return
-    i = OWN.index(core % 8)
-    o = core // 8
-    g.wait_ge(T.sem.got, sum(8 if r == o else 1 for r in range(n - 1)))
-    sent = 0
-    for call in sched(o):
+
+    if core % 8 in REL:
+        i = REL.index(core % 8)
+        g.wait_ge(T.sem.relin, 8)
         trs = []
-        for r, m in call:
-            rid, pid, se = topo.addr(T.cores[r])
-            sent += bits(m)
-            if r == 1:
-                trs.append(RemoteDMATransfer(dst_ids=[DstId(rid=rid, pnc=pid)], dma_engine_mask=m,
-                                             remote_sem=arrived[i], src=gath[i][0], dst=land[i][o]))
-            else:
-                trs.append(RemoteDMATransfer(dst_ids=[DstId(rid=rid, pnc=pid)], dma_engine_mask=m,
-                                             remote_sem=arrived[i], srcs=[gath[i][j] for j in range(r)],
-                                             dsts=[land[i][o]], alu_op=1))
+        for s, r in enumerate(relayed(o)):
+            trs.append(RemoteDMATransfer(dst_ids=to(T.cores[r]), dma_engine_mask=[LO, HI][s],
+                                         remote_sem=arrived[i], src=rel[i][s], dst=land[i][o]))
         g.remote_dma_fused(trs, local_sem=T.sem.sent)
-    g.wait_ge(T.sem.sent, sent)
+        g.wait_ge(T.sem.sent, 8)

@@ -3,7 +3,7 @@ from concourse.mybir import AluOpType
 
 OWN = [3, 6, 7]
 REL = [0, 4, 5]
-WID = [86, 86, 84]
+WID = [96, 86, 74]
 ROWS = [w // 2 for w in WID]
 BASE = [sum(ROWS[:i]) for i in range(len(WID))]
 K = len(OWN)
@@ -12,10 +12,10 @@ for i in range(K):
     SCRATCH["xd%d" % i] = ("dram", [8, 128, WID[i]], "bfloat16")
     SCRATCH["gath%d" % i] = ("dram", [7, 128, WID[i]], "bfloat16")
     SCRATCH["land%d" % i] = ("dram", [8, 128, WID[i]], "bfloat16")
-    SCRATCH["rel%d" % i] = ("dram", [2, 128, WID[i]], "bfloat16")
+    SCRATCH["rel%d" % i] = ("dram", [128, WID[i]], "bfloat16")
 SEMAPHORES = (["copied", "added", "got", "sent", "relin"] + ["loaded%d" % i for i in range(K)]
               + ["arrived%d" % i for i in range(K)])
-LO, HI = 0x0F, 0xF0
+LO, HI, UP = 0x0F, 0xF0, 0xFF00
 
 
 def bits(m):
@@ -23,22 +23,20 @@ def bits(m):
 
 
 def relayed(o):
-    same = [r for r in range(7, 0, -1) if r % 2 == o % 2 and r != o]
-    if o % 2 == 1 and same[0] == 7:
-        same = same[1:]
-    return same[:2]
+    if o % 2 == 0:
+        return 6 if o != 6 else 4
+    return 7 if o != 7 else 5
 
 
 def sched(o):
     rl = relayed(o)
-    d = [r for r in range(7, 0, -1) if r != o and r not in rl]
-    a = [(d[0], LO, None), (d[1], HI, None), (rl[0], 0x0F00, 0), (rl[1], 0xF000, 1)]
-    b = [(d[2], HI, None), (d[3], LO, None)]
+    d = [r for r in range(7, 0, -1) if r != o and r != rl]
+    calls = [[(d[0], LO, False), (d[1], HI, False), (rl, UP, True)], [(d[2], HI, False), (d[3], LO, False)],
+             [(d[4], HI, False)]]
     if o >= 1:
-        b.append((o, 0xFF00, None))
-    calls = [a, b]
-    if len(d) > 4:
-        calls.append([(d[4], HI, None)])
+        calls[1].append((o, UP, False))
+    if len(d) > 5:
+        calls[2].append((d[5], LO, False))
     return calls
 
 
@@ -67,7 +65,7 @@ def rank_program(g, core, T, topo):
                 trs = []
                 eng = [e for e in range(8) if e != i]
                 for c in range(8):
-                    m = 0xFF00 if c == o else 1 << eng.pop(0)
+                    m = UP if c == o else 1 << eng.pop(0)
                     sent += bits(m)
                     trs.append(RemoteDMATransfer(dst_ids=to(8 * c + OWN[i]), dma_engine_mask=m,
                                                  remote_sem=T.sem.got, src=xd[i][c], dst=gath[i][rank]))
@@ -75,7 +73,7 @@ def rank_program(g, core, T, topo):
         g.dma_start(T.y[:], T.x[:]).then_inc(T.sem.copied, 16)
         g.wait_ge(T.sem.copied, 16)
         if rank > 0:
-            need = sum(bits(m) for c in range(8) for call in sched(c) for r, m, s in call if r == rank)
+            need = sum(bits(m) for c in range(8) for call in sched(c) for r, m, q in call if r == rank)
             for i in range(K):
                 g.wait_ge(arrived[i], need)
                 g.dma_start(T.y[BASE[i]:BASE[i] + ROWS[i], :], land[i][:], accum_op=AluOpType.add,
@@ -91,12 +89,12 @@ def rank_program(g, core, T, topo):
         sent = 0
         for call in sched(o):
             trs = []
-            for r, m, s in call:
+            for r, m, q in call:
                 sent += bits(m)
-                if s is None:
-                    where, sem, out = to(T.cores[r]), arrived[i], land[i][o]
+                if q:
+                    where, sem, out = to(8 * o + REL[i]), T.sem.relin, rel[i][:]
                 else:
-                    where, sem, out = to(8 * o + REL[i]), T.sem.relin, rel[i][s]
+                    where, sem, out = to(T.cores[r]), arrived[i], land[i][o]
                 if r == 1:
                     trs.append(RemoteDMATransfer(dst_ids=where, dma_engine_mask=m, remote_sem=sem,
                                                  src=gath[i][0], dst=out))
@@ -109,10 +107,7 @@ def rank_program(g, core, T, topo):
 
     if core % 8 in REL:
         i = REL.index(core % 8)
+        rid, pid, se = topo.addr(T.cores[relayed(o)])
         g.wait_ge(T.sem.relin, 8)
-        trs = []
-        for s, r in enumerate(relayed(o)):
-            trs.append(RemoteDMATransfer(dst_ids=to(T.cores[r]), dma_engine_mask=[LO, HI][s],
-                                         remote_sem=arrived[i], src=rel[i][s], dst=land[i][o]))
-        g.remote_dma_fused(trs, local_sem=T.sem.sent)
+        g.remote_dma(land[i][o], rel[i][:], arrived[i], T.sem.sent, pid, rid, 0xFF)
         g.wait_ge(T.sem.sent, 8)

from concourse.bass import DstId, RemoteDMATransfer
from concourse.mybir import AluOpType

OWN = [3, 6, 7]
REL = [0, 4, 5]
WID = [96, 86, 74]
ROWS = [w // 2 for w in WID]
BASE = [sum(ROWS[:i]) for i in range(len(WID))]
K = len(OWN)
SCRATCH = {}
for i in range(K):
    SCRATCH["xd%d" % i] = ("dram", [8, 128, WID[i]], "bfloat16")
    SCRATCH["gath%d" % i] = ("dram", [7, 128, WID[i]], "bfloat16")
    SCRATCH["land%d" % i] = ("dram", [8, 128, WID[i]], "bfloat16")
    SCRATCH["rel%d" % i] = ("dram", [128, WID[i]], "bfloat16")
SEMAPHORES = (["copied", "added", "got", "sent", "relin"] + ["loaded%d" % i for i in range(K)]
              + ["arrived%d" % i for i in range(K)])
LO, HI, UP = 0x0F, 0xF0, 0xFF00


def bits(m):
    return bin(m).count("1")


def relayed(o):
    if o % 2 == 0:
        return 6 if o != 6 else 4
    return 7 if o != 7 else 5


def sched(o):
    rl = relayed(o)
    d = [r for r in range(7, 0, -1) if r != o and r != rl]
    calls = [[(d[0], LO, False), (d[1], HI, False), (rl, UP, True)], [(d[2], HI, False), (d[3], LO, False)],
             [(d[4], HI, False)]]
    if o >= 1:
        calls[1].append((o, UP, False))
    if len(d) > 5:
        calls[2].append((d[5], LO, False))
    return calls


def rank_program(g, core, T, topo):
    rank = T.rank_of(core)
    n = len(T.cores)
    xd = [T.xd0, T.xd1, T.xd2]
    gath = [T.gath0, T.gath1, T.gath2]
    land = [T.land0, T.land1, T.land2]
    rel = [T.rel0, T.rel1, T.rel2]
    loaded = [T.sem.loaded0, T.sem.loaded1, T.sem.loaded2]
    arrived = [T.sem.arrived0, T.sem.arrived1, T.sem.arrived2]
    o = topo.chip(core)

    def to(dst):
        rid, pid, se = topo.addr(dst)
        return [DstId(rid=rid, pnc=pid)]

    if rank is not None:
        sent = 0
        if rank < n - 1:
            for i in range(K):
                g.dma_start(xd[i][:], T.x[BASE[i]:BASE[i] + ROWS[i], :]).then_inc(loaded[i], 16)
            for i in range(K):
                g.wait_ge(loaded[i], 16)
                trs = []
                eng = [e for e in range(8) if e != i]
                for c in range(8):
                    m = UP if c == o else 1 << eng.pop(0)
                    sent += bits(m)
                    trs.append(RemoteDMATransfer(dst_ids=to(8 * c + OWN[i]), dma_engine_mask=m,
                                                 remote_sem=T.sem.got, src=xd[i][c], dst=gath[i][rank]))
                g.remote_dma_fused(trs, local_sem=T.sem.sent)
        g.dma_start(T.y[:], T.x[:]).then_inc(T.sem.copied, 16)
        g.wait_ge(T.sem.copied, 16)
        if rank > 0:
            need = sum(bits(m) for c in range(8) for call in sched(c) for r, m, q in call if r == rank)
            for i in range(K):
                g.wait_ge(arrived[i], need)
                g.dma_start(T.y[BASE[i]:BASE[i] + ROWS[i], :], land[i][:], accum_op=AluOpType.add,
                            max_dma_last_dim=4096).then_inc(T.sem.added, 16)
            g.wait_ge(T.sem.added, 16 * K)
        if sent:
            g.wait_ge(T.sem.sent, sent)
        return

    if core % 8 in OWN:
        i = OWN.index(core % 8)
        g.wait_ge(T.sem.got, sum(8 if r == o else 1 for r in range(n - 1)))
        sent = 0
        for call in sched(o):
            trs = []
            for r, m, q in call:
                sent += bits(m)
                if q:
                    where, sem, out = to(8 * o + REL[i]), T.sem.relin, rel[i][:]
                else:
                    where, sem, out = to(T.cores[r]), arrived[i], land[i][o]
                if r == 1:
                    trs.append(RemoteDMATransfer(dst_ids=where, dma_engine_mask=m, remote_sem=sem,
                                                 src=gath[i][0], dst=out))
                else:
                    trs.append(RemoteDMATransfer(dst_ids=where, dma_engine_mask=m, remote_sem=sem,
                                                 srcs=[gath[i][j] for j in range(r)], dsts=[out], alu_op=1))
            g.remote_dma_fused(trs, local_sem=T.sem.sent)
        g.wait_ge(T.sem.sent, sent)
        return

    if core % 8 in REL:
        i = REL.index(core % 8)
        rid, pid, se = topo.addr(T.cores[relayed(o)])
        g.wait_ge(T.sem.relin, 8)
        g.remote_dma(land[i][o], rel[i][:], arrived[i], T.sem.sent, pid, rid, 0xFF)
        g.wait_ge(T.sem.sent, 8)
